import numpy as np
import ml_dtypes


def mxq(x, axis, fmt="e4m3"):
    dtype, down = {"e4m3": (ml_dtypes.float8_e4m3fn, 7), "e5m2": (ml_dtypes.float8_e5m2, 14)}[fmt]
    v = np.moveaxis(np.asarray(x, np.float32).astype(ml_dtypes.bfloat16).astype(np.float64), axis, -1)
    blocks = v.reshape(v.shape[:-1] + (-1, 32))
    amax = np.abs(blocks).max(-1, keepdims=True)
    byte = np.maximum(np.where(amax > 0, np.frexp(amax)[1] - 1 + 127, 0) - down, 1)
    scale = np.exp2(byte - 127.0)
    codes = (blocks / scale).astype(np.float32).astype(dtype).astype(np.float64)
    return np.moveaxis((codes * scale).reshape(v.shape), -1, axis)


WIDE = False


def mx_kscale(k):
    if not WIDE:
        return np.ones(k)
    levels = np.array([10, -10, 5, -5, 0])
    if k % 512:
        return np.exp2(np.random.permutation(np.resize(levels, k // 32))).repeat(32)
    a = np.empty((k // 512, 16))
    for p in range(k // 512):
        a[p, :8] = np.random.permutation(np.resize(levels, 8))
        for g in range(8):
            far = levels[np.abs(levels - a[p, g]) >= 10]
            a[p, g + 8] = far[np.random.randint(len(far))]
    return np.exp2(a.ravel()).repeat(32)


def f64(x):
    return np.asarray(x).astype(np.float64)


def striped(idx):
    return np.tile(idx.reshape(-1, 16).T, (8, 1)).astype(np.uint16)


def unstriped(offs):
    return offs[:16].T.reshape(-1).astype(np.int64)


def pack_weight(w):
    k, n = w.shape
    w = f64(np.asarray(w, np.float32).astype(ml_dtypes.bfloat16)).reshape(k // 32, 32, n)
    amax = np.abs(w).max(1)
    byte = np.clip(np.where(amax > 0, np.frexp(amax)[1] - 1 + 127 - 7, 1), 1, 254)
    scaled = (w * np.exp2(127.0 - byte)[:, None, :]).reshape(k, n).astype(np.float32)
    words = np.ascontiguousarray(scaled.reshape(k // 512, 128, 4, n).transpose(0, 1, 3, 2)).astype(ml_dtypes.float8_e4m3fn).view(np.uint8)
    return words, np.ascontiguousarray(byte.astype(np.uint8).reshape(k // 512, 16, n))


def unpack_weight(words, scales):
    g, p, n, _ = words.shape
    vals = np.ascontiguousarray(words).view(ml_dtypes.float8_e4m3fn).astype(np.float64) * np.repeat(np.exp2(scales.astype(np.float64) - 127.0), 8, axis=1)[..., None]
    return vals.transpose(0, 1, 3, 2).reshape(g * 512, n)


def relu2(v):
    return np.maximum(v, 0.0) ** 2


K, T, S, H, N = 512, 2048, 1024, 1024, 256


def setup_inputs():
    n = np.random.standard_normal
    s = mx_kscale(K)[:, None]
    u = mx_kscale(H)
    packed = pack_weight(n((K, T)) * s)
    return {
        "x_words": packed[0],
        "x_scales": packed[1],
        "w1": (n((K, H)) / np.sqrt(K) / s * u).astype(np.float32),
        "w2": (n((H, N)) / np.sqrt(H) / u[:, None] ** 2).astype(np.float32),
        "gate": np.tile(np.random.uniform(0.2, 1.0, S), (N, 1)).astype(np.float32),
        "offs": striped(np.random.permutation(T)[:S]),
    }


def reference(x_words, x_scales, w1, w2, gate, offs):
    idx = unstriped(offs)
    xq = unpack_weight(x_words, x_scales)[:, idx]
    h = relu2(mxq(f64(w1), 0, "e4m3").T @ xq)
    y = mxq(f64(w2), 0, "e4m3").T @ mxq(h, 0, "e4m3")
    out = np.zeros((N, T))
    out[:, idx] = f64(gate) * y
    return out

@@ -1,0 +1,176 @@
+from contextlib import ExitStack
+
+import concourse.mybir as mybir
+
+K, T, S, H, N = 512, 2048, 1024, 1024, 256
+FLOPS = 2 * S * (K * H + H * N)
+
+F32 = mybir.dt.float32
+BF16 = mybir.dt.bfloat16
+I32 = mybir.dt.int32
+U32 = mybir.dt.uint32
+U16 = mybir.dt.uint16
+U8 = mybir.dt.uint8
+FP8X4 = mybir.dt.float8_e4m3fn_x4
+ACT = mybir.ActivationFunctionType
+ALU = mybir.AluOpType
+
+P = 128
+PACK = 4
+PASS = P * PACK
+PASSES = H // PASS
+CHUNK = 256
+CHUNKS = S // CHUNK
+UNIT = 128
+ROW_TILES = N // P
+LIST_ROWS = 16
+
+
+def tile_picked_depth_mlp_relu2_sub_p_kernel(tc, x_words, x_scales, w1, w2, gate, offs, out):
+    nc = tc.nc
+    with ExitStack() as ctx:
+        keep = ctx.enter_context(tc.tile_pool(name="keep", bufs=1))
+        ring = ctx.enter_context(tc.tile_pool(name="ring", bufs=4))
+        psum_h = ctx.enter_context(tc.psum_pool(name="psum_h", bufs=6))
+        psum_y = ctx.enter_context(tc.psum_pool(name="psum_y", bufs=2))
+
+        offsets = keep.tile([P, S // LIST_ROWS], U16, name="offsets")
+        nc.sync.dma_start(offsets[:], offs)
+
+        all_scales = keep.tile([P, T], U8, name="all_scales", align_bytes=64)
+        nc.gpsimd.memset(all_scales[:].bitcast(I32), 0)
+
+        warm_in = keep.tile([P, 8], F32, name="warm_in")
+        warm_out = keep.tile([P, 8], F32, name="warm_out")
+        nc.vector.memset(warm_in[:], 0.0)
+        nc.scalar.activation(warm_out[:], warm_in[:], ACT.Relu)
+
+        w1_rows = w1.rearrange("(p j) c -> p j c", j=PACK)
+        half = PASS // 2
+        w1_first = []
+        for u in range(2):
+            raw = keep.tile([P, PACK, half], F32, name=f"w1_first{u}")
+            nc.sync.dma_start(raw[:], w1_rows[:, :, u * half : (u + 1) * half])
+            w1_first.append(raw)
+            if u == 0:
+                for q in range(4):
+                    nc.sync.dma_start(all_scales[32 * q : 32 * q + 4, :].bitcast(I32), x_scales[0, 4 * q : 4 * q + 4, :].bitcast(I32))
+        all_words = keep.tile([P, T], I32, name="all_words", align_bytes=64)
+        nc.sync.dma_start(all_words[:], x_words[0].rearrange("p c r -> p (c r)").bitcast(I32))
+        w1_second = keep.tile([P, PACK, PASS], F32, name="w1_second")
+        nc.sync.dma_start(w1_second[:], w1_rows[:, :, PASS : 2 * PASS])
+        w2_raw = []
+        for g in range(PASSES):
+            raw = keep.tile([P, PACK, N], F32, name=f"w2_raw{g}")
+            nc.sync.dma_start(raw[:], w2[g * PASS : (g + 1) * PASS, :].rearrange("(p j) n -> p j n", j=PACK))
+            w2_raw.append(raw)
+        gates = keep.tile([P, S], F32, name="gates")
+        nc.sync.dma_start(gates[:], gate[0:P, :])
+
+        windows = []
+        for m in range(ROW_TILES):
+            window = keep.tile([P, T], F32, name=f"window{m}")
+            nc.vector.memset(window[:], 0.0)
+            windows.append(window)
+
+        picked_scales = keep.tile([P, S], U8, name="picked_scales", align_bytes=64)
+        nc.vector.tensor_copy(picked_scales[:], all_scales[:].indirect(offsets[:]))
+
+        w1_grouped = [keep.tile([P, PACK, P, PACK], BF16, name=f"w1_grouped{g}", align_bytes=64) for g in range(PASSES)]
+        w1_codes = [keep.tile([P, PASS], U32, name=f"w1_codes{g}", align_bytes=64) for g in range(PASSES)]
+        w1_planes = [keep.tile([P, PASS], U8, name=f"w1_planes{g}", align_bytes=64) for g in range(PASSES)]
+
+        def quantize_w1(g):
+            nc.vector.quantize_mx(
+                out=w1_codes[g][:].bitcast(FP8X4),
+                scales=w1_planes[g][:],
+                in_=w1_grouped[g][:].rearrange("p t m j -> p (t m j)"),
+            )
+
+        for u in range(2):
+            nc.scalar.copy(
+                w1_grouped[0][:, :, u * (P // 2) : (u + 1) * (P // 2), :].rearrange("p t m j -> p m t j"),
+                w1_first[u][:].rearrange("p j (m t) -> p m t j", t=PACK),
+            )
+        quantize_w1(0)
+
+        def chunk_offsets(c):
+            return offsets[:, c * (CHUNK // LIST_ROWS) : (c + 1) * (CHUNK // LIST_ROWS)]
+
+        picked_words = []
+        for c in range(CHUNKS):
+            words = keep.tile([P, CHUNK], U32, name=f"picked_words{c}", align_bytes=64)
+            nc.vector.tensor_copy(words[:], all_words[:].bitcast(U32).indirect(chunk_offsets(c)))
+            picked_words.append(words)
+
+        nc.vector.tensor_copy(
+            w1_grouped[1][:].rearrange("p t m j -> p m t j"),
+            w1_second[:].rearrange("p j (m t) -> p m t j", t=PACK),
+        )
+        quantize_w1(1)
+
+        w2_codes, w2_planes = [], []
+        for g in range(PASSES):
+            grouped = keep.tile([P, N, PACK], BF16, name=f"w2_grouped{g}", align_bytes=64)
+            nc.vector.tensor_copy(grouped[:], w2_raw[g][:].rearrange("p j n -> p n j"))
+            codes = keep.tile([P, N], U32, name=f"w2_codes{g}", align_bytes=64)
+            plane = keep.tile([P, N], U8, name=f"w2_plane{g}", align_bytes=64)
+            nc.vector.quantize_mx(out=codes[:].bitcast(FP8X4), scales=plane[:], in_=grouped[:].rearrange("p n j -> p (n j)"))
+            w2_codes.append(codes)
+            w2_planes.append(plane)
+
+        def put_back(c, m, y, product):
+            nc.vector.tensor_tensor(product[:], y[:, m, :], gates[:, c * CHUNK : (c + 1) * CHUNK], ALU.mult)
+            nc.vector.tensor_copy(windows[m][:].indirect(chunk_offsets(c)), product[:])
+
+        held = None
+        for c in range(CHUNKS):
+            h_codes, h_planes = [], []
+            for g in range(PASSES):
+                codes = keep.tile([P, CHUNK], U32, name=f"h_codes{c}_{g}", align_bytes=64)
+                plane = keep.tile([P, CHUNK], U8, name=f"h_plane{c}_{g}", align_bytes=64)
+                for a in range(CHUNK // UNIT):
+                    cols = slice(a * UNIT, (a + 1) * UNIT)
+                    entries = slice(c * CHUNK + a * UNIT, c * CHUNK + (a + 1) * UNIT)
+                    pre = psum_h.tile([P, PACK, UNIT], F32, name="pre")
+                    for t in range(PACK):
+                        nc.tensor.matmul_mx(
+                            out=pre[:, t, :],
+                            lhsT=w1_codes[g][:, t * P : (t + 1) * P].bitcast(FP8X4),
+                            lhsT_scale=w1_planes[g][:, t * P : (t + 1) * P],
+                            rhs=picked_words[c][:, cols].bitcast(FP8X4),
+                            rhs_scale=picked_scales[:, entries],
+                            start=True,
+                            stop=True,
+                        )
+                    positive = ring.tile([P, UNIT, PACK], F32, name="positive")
+                    nc.scalar.activation(positive[:], pre[:].rearrange("p t n -> p n t"), ACT.Relu)
+                    if g == PASSES - 1 and a == CHUNK // UNIT - 1:
+                        hidden = keep.tile([P, UNIT * PACK], BF16, name="hidden_last", tag="shared", align_bytes=64)
+                    else:
+                        hidden = keep.tile([P, UNIT * PACK], BF16, name=f"hidden{c}_{g}_{a}", align_bytes=64)
+                    nc.scalar.activation(hidden[:], positive[:].rearrange("p n t -> p (n t)"), ACT.Square)
+                    nc.vector.quantize_mx(out=codes[:, cols].bitcast(FP8X4), scales=plane[:, cols], in_=hidden[:])
+                h_codes.append(codes)
+                h_planes.append(plane)
+
+            y = psum_y.tile([P, ROW_TILES, CHUNK], F32, name="y")
+            for m in range(ROW_TILES):
+                for g in range(PASSES):
+                    nc.tensor.matmul_mx(
+                        out=y[:, m, :],
+                        lhsT=w2_codes[g][:, m * P : (m + 1) * P].bitcast(FP8X4),
+                        lhsT_scale=w2_planes[g][:, m * P : (m + 1) * P],
+                        rhs=h_codes[g][:].bitcast(FP8X4),
+                        rhs_scale=h_planes[g][:],
+                        start=(g == 0),
+                        stop=(g == PASSES - 1),
+                    )
+            if held is not None:
+                put_back(c - 1, 1, held, keep.tile([P, CHUNK], F32, name="product_held", tag="shared", align_bytes=64))
+            put_back(c, 0, y, ring.tile([P, CHUNK], F32, name="product"))
+            held = y
+        put_back(CHUNKS - 1, 1, held, ring.tile([P, CHUNK], F32, name="product"))
+
+        for m in range(ROW_TILES):
+            nc.sync.dma_start(out[m * P : (m + 1) * P, :], windows[m][:])

@@ -31,14 +31,15 @@ def tile_picked_depth_mlp_relu2_sub_p_kernel(tc, x_words, x_scales, w1, w2, gate
     with ExitStack() as ctx:
         keep = ctx.enter_context(tc.tile_pool(name="keep", bufs=1))
         ring = ctx.enter_context(tc.tile_pool(name="ring", bufs=4))
-        psum_h = ctx.enter_context(tc.psum_pool(name="psum_h", bufs=6))
-        psum_y = ctx.enter_context(tc.psum_pool(name="psum_y", bufs=2))
+        psum_h = ctx.enter_context(tc.psum_pool(name="psum_h", bufs=5))
+        psum_y = ctx.enter_context(tc.psum_pool(name="psum_y", bufs=1))
 
         offsets = keep.tile([P, S // LIST_ROWS], U16, name="offsets")
         nc.sync.dma_start(offsets[:], offs)
 
         all_scales = keep.tile([P, T], U8, name="all_scales", align_bytes=64)
-        nc.gpsimd.memset(all_scales[:].bitcast(I32), 0)
+        nc.gpsimd.memset(all_scales[:, 0 : T // 2].bitcast(I32), 0)
+        nc.vector.memset(all_scales[:, T // 2 : T].bitcast(I32), 0)
 
         warm_in = keep.tile([P, 8], F32, name="warm_in")
         warm_out = keep.tile([P, 8], F32, name="warm_out")
@@ -57,11 +58,14 @@ def tile_picked_depth_mlp_relu2_sub_p_kernel(tc, x_words, x_scales, w1, w2, gate
                     nc.sync.dma_start(all_scales[32 * q : 32 * q + 4, :].bitcast(I32), x_scales[0, 4 * q : 4 * q + 4, :].bitcast(I32))
         all_words = keep.tile([P, T], I32, name="all_words", align_bytes=64)
         nc.sync.dma_start(all_words[:], x_words[0].rearrange("p c r -> p (c r)").bitcast(I32))
-        w1_second = keep.tile([P, PACK, PASS], F32, name="w1_second")
-        nc.sync.dma_start(w1_second[:], w1_rows[:, :, PASS : 2 * PASS])
+        w1_second = []
+        for u in range(2):
+            raw = keep.tile([P, PACK, half], F32, name=f"w1_second{u}", tag=f"w1_second{u}", align_bytes=64)
+            nc.sync.dma_start(raw[:], w1_rows[:, :, PASS + u * half : PASS + (u + 1) * half])
+            w1_second.append(raw)
         w2_raw = []
         for g in range(PASSES):
-            raw = keep.tile([P, PACK, N], F32, name=f"w2_raw{g}")
+            raw = keep.tile([P, PACK, N], F32, name=f"w2_raw{g}", tag=f"w2_raw{g}", align_bytes=64)
             nc.sync.dma_start(raw[:], w2[g * PASS : (g + 1) * PASS, :].rearrange("(p j) n -> p j n", j=PACK))
             w2_raw.append(raw)
         gates = keep.tile([P, S], F32, name="gates")
@@ -97,38 +101,51 @@ def tile_picked_depth_mlp_relu2_sub_p_kernel(tc, x_words, x_scales, w1, w2, gate
         def chunk_offsets(c):
             return offsets[:, c * (CHUNK // LIST_ROWS) : (c + 1) * (CHUNK // LIST_ROWS)]
 
-        picked_words = []
-        for c in range(CHUNKS):
-            words = keep.tile([P, CHUNK], U32, name=f"picked_words{c}", align_bytes=64)
-            nc.vector.tensor_copy(words[:], all_words[:].bitcast(U32).indirect(chunk_offsets(c)))
-            picked_words.append(words)
+        picked_words = {}
 
-        nc.vector.tensor_copy(
-            w1_grouped[1][:].rearrange("p t m j -> p m t j"),
-            w1_second[:].rearrange("p j (m t) -> p m t j", t=PACK),
-        )
+        def pick_words(c, tag):
+            words = keep.tile([P, CHUNK], U32, name=f"picked_words{c}", tag=tag, align_bytes=64)
+            nc.vector.tensor_copy(words[:], all_words[:].bitcast(U32).indirect(chunk_offsets(c)))
+            picked_words[c] = words
+
+        pick_words(0, "picked_words0")
+        pick_words(1, "picked_words1")
+        for u in range(2):
+            nc.vector.tensor_copy(
+                w1_grouped[1][:, :, u * (P // 2) : (u + 1) * (P // 2), :].rearrange("p t m j -> p m t j"),
+                w1_second[u][:].rearrange("p j (m t) -> p m t j", t=PACK),
+            )
         quantize_w1(1)
+        pick_words(2, "picked_words2")
 
         w2_codes, w2_planes = [], []
         for g in range(PASSES):
             grouped = keep.tile([P, N, PACK], BF16, name=f"w2_grouped{g}", align_bytes=64)
-            nc.vector.tensor_copy(grouped[:], w2_raw[g][:].rearrange("p j n -> p n j"))
+            nc.vector.tensor_copy(
+                grouped[:].rearrange("p (n i) j -> p n j i", i=4),
+                w2_raw[g][:].rearrange("p j (n i) -> p n j i", i=4),
+            )
             codes = keep.tile([P, N], U32, name=f"w2_codes{g}", align_bytes=64)
             plane = keep.tile([P, N], U8, name=f"w2_plane{g}", align_bytes=64)
             nc.vector.quantize_mx(out=codes[:].bitcast(FP8X4), scales=plane[:], in_=grouped[:].rearrange("p n j -> p (n j)"))
             w2_codes.append(codes)
             w2_planes.append(plane)
+        pick_words(3, "w2_raw1")
 
-        def put_back(c, m, y, product):
-            nc.vector.tensor_tensor(product[:], y[:, m, :], gates[:, c * CHUNK : (c + 1) * CHUNK], ALU.mult)
-            nc.vector.tensor_copy(windows[m][:].indirect(chunk_offsets(c)), product[:])
+        def put_back(c, m, y, staged):
+            nc.scalar.copy(staged[:], y[:])
+            nc.vector.tensor_tensor(windows[m][:].indirect(chunk_offsets(c)), staged[:], gates[:, c * CHUNK : (c + 1) * CHUNK], ALU.mult)
 
+        on_vector = [[0, 512], [512, 0], [512, 0], [512, 0]]
+        width = CHUNK * PACK
         held = None
         for c in range(CHUNKS):
-            h_codes, h_planes = [], []
+            ys = [psum_y.tile([P, CHUNK], F32, name="y0", bufs=1), psum_y.tile([P, CHUNK], F32, name="y1", bufs=2)]
             for g in range(PASSES):
-                codes = keep.tile([P, CHUNK], U32, name=f"h_codes{c}_{g}", align_bytes=64)
-                plane = keep.tile([P, CHUNK], U8, name=f"h_plane{c}_{g}", align_bytes=64)
+                if g == PASSES - 1:
+                    positive = keep.tile([P, CHUNK, PACK], F32, name="positive_last", tag=f"shared{c % 2}")
+                else:
+                    positive = ring.tile([P, CHUNK, PACK], F32, name="positive")
                 for a in range(CHUNK // UNIT):
                     cols = slice(a * UNIT, (a + 1) * UNIT)
                     entries = slice(c * CHUNK + a * UNIT, c * CHUNK + (a + 1) * UNIT)
@@ -143,34 +160,32 @@ def tile_picked_depth_mlp_relu2_sub_p_kernel(tc, x_words, x_scales, w1, w2, gate
                             start=True,
                             stop=True,
                         )
-                    positive = ring.tile([P, UNIT, PACK], F32, name="positive")
-                    nc.scalar.activation(positive[:], pre[:].rearrange("p t n -> p n t"), ACT.Relu)
-                    if g == PASSES - 1 and a == CHUNK // UNIT - 1:
-                        hidden = keep.tile([P, UNIT * PACK], BF16, name="hidden_last", tag="shared", align_bytes=64)
-                    else:
-                        hidden = keep.tile([P, UNIT * PACK], BF16, name=f"hidden{c}_{g}_{a}", align_bytes=64)
-                    nc.scalar.activation(hidden[:], positive[:].rearrange("p n t -> p (n t)"), ACT.Square)
-                    nc.vector.quantize_mx(out=codes[:, cols].bitcast(FP8X4), scales=plane[:, cols], in_=hidden[:])
-                h_codes.append(codes)
-                h_planes.append(plane)
-
-            y = psum_y.tile([P, ROW_TILES, CHUNK], F32, name="y")
-            for m in range(ROW_TILES):
-                for g in range(PASSES):
+                    nc.scalar.activation(positive[:, cols, :], pre[:].rearrange("p t n -> p n t"), ACT.Relu)
+                flat = positive[:].rearrange("p n t -> p (n t)")
+                hidden = keep.tile([P, width], BF16, name=f"hidden{c}_{g}", align_bytes=64)
+                share = on_vector[c][g]
+                if share > 0:
+                    nc.vector.tensor_tensor(hidden[:, 0:share], flat[:, 0:share], flat[:, 0:share], ALU.mult)
+                if share < width:
+                    nc.scalar.activation(hidden[:, share:width], flat[:, share:width], ACT.Square)
+                codes = keep.tile([P, CHUNK], U32, name=f"h_codes{c}_{g}", align_bytes=64)
+                plane = keep.tile([P, CHUNK], U8, name=f"h_plane{c}_{g}", align_bytes=64)
+                nc.vector.quantize_mx(out=codes[:].bitcast(FP8X4), scales=plane[:], in_=hidden[:])
+                for m in range(ROW_TILES):
                     nc.tensor.matmul_mx(
-                        out=y[:, m, :],
+                        out=ys[m][:],
                         lhsT=w2_codes[g][:, m * P : (m + 1) * P].bitcast(FP8X4),
                         lhsT_scale=w2_planes[g][:, m * P : (m + 1) * P],
-                        rhs=h_codes[g][:].bitcast(FP8X4),
-                        rhs_scale=h_planes[g][:],
+                        rhs=codes[:].bitcast(FP8X4),
+                        rhs_scale=plane[:],
                         start=(g == 0),
                         stop=(g == PASSES - 1),
                     )
             if held is not None:
-                put_back(c - 1, 1, held, keep.tile([P, CHUNK], F32, name="product_held", tag="shared", align_bytes=64))
-            put_back(c, 0, y, ring.tile([P, CHUNK], F32, name="product"))
-            held = y
-        put_back(CHUNKS - 1, 1, held, ring.tile([P, CHUNK], F32, name="product"))
+                put_back(c - 1, 1, held, keep.tile([P, CHUNK], F32, name="staged_held", tag=f"shared{c % 2}"))
+            put_back(c, 0, ys[0], ring.tile([P, CHUNK], F32, name="staged"))
+            held = ys[1]
+        put_back(CHUNKS - 1, 1, held, ring.tile([P, CHUNK], F32, name="staged"))
 
         for m in range(ROW_TILES):
             nc.sync.dma_start(out[m * P : (m + 1) * P, :], windows[m][:])

@@ -41,10 +41,6 @@ def tile_picked_depth_mlp_relu2_sub_p_kernel(tc, x_words, x_scales, w1, w2, gate
         nc.gpsimd.memset(all_scales[:, 0 : T // 2].bitcast(I32), 0)
         nc.vector.memset(all_scales[:, T // 2 : T].bitcast(I32), 0)
 
-        warm_in = keep.tile([P, 8], F32, name="warm_in")
-        warm_out = keep.tile([P, 8], F32, name="warm_out")
-        nc.vector.memset(warm_in[:], 0.0)
-        nc.scalar.activation(warm_out[:], warm_in[:], ACT.Relu)
 
         w1_rows = w1.rearrange("(p j) c -> p j c", j=PACK)
         half = PASS // 2
@@ -93,8 +89,8 @@ def tile_picked_depth_mlp_relu2_sub_p_kernel(tc, x_words, x_scales, w1, w2, gate
 
         for u in range(2):
             nc.scalar.copy(
-                w1_grouped[0][:, :, u * (P // 2) : (u + 1) * (P // 2), :].rearrange("p t m j -> p m t j"),
-                w1_first[u][:].rearrange("p j (m t) -> p m t j", t=PACK),
+                w1_grouped[0][:, :, u * (P // 2) : (u + 1) * (P // 2), :].rearrange("p t m j -> p m j t"),
+                w1_first[u][:].rearrange("p j (m t) -> p m j t", t=PACK),
             )
         quantize_w1(0)
 
@@ -112,8 +108,8 @@ def tile_picked_depth_mlp_relu2_sub_p_kernel(tc, x_words, x_scales, w1, w2, gate
         pick_words(1, "picked_words1")
         for u in range(2):
             nc.vector.tensor_copy(
-                w1_grouped[1][:, :, u * (P // 2) : (u + 1) * (P // 2), :].rearrange("p t m j -> p m t j"),
-                w1_second[u][:].rearrange("p j (m t) -> p m t j", t=PACK),
+                w1_grouped[1][:, :, u * (P // 2) : (u + 1) * (P // 2), :].rearrange("p t m j -> p m j t"),
+                w1_second[u][:].rearrange("p j (m t) -> p m j t", t=PACK),
             )
         quantize_w1(1)
         pick_words(2, "picked_words2")

from contextlib import ExitStack

import concourse.mybir as mybir

K, T, S, H, N = 512, 2048, 1024, 1024, 256
FLOPS = 2 * S * (K * H + H * N)

F32 = mybir.dt.float32
BF16 = mybir.dt.bfloat16
I32 = mybir.dt.int32
U32 = mybir.dt.uint32
U16 = mybir.dt.uint16
U8 = mybir.dt.uint8
FP8X4 = mybir.dt.float8_e4m3fn_x4
ACT = mybir.ActivationFunctionType
ALU = mybir.AluOpType

P = 128
PACK = 4
PASS = P * PACK
PASSES = H // PASS
CHUNK = 256
CHUNKS = S // CHUNK
UNIT = 128
ROW_TILES = N // P
LIST_ROWS = 16


def tile_picked_depth_mlp_relu2_sub_p_kernel(tc, x_words, x_scales, w1, w2, gate, offs, out):
    nc = tc.nc
    with ExitStack() as ctx:
        keep = ctx.enter_context(tc.tile_pool(name="keep", bufs=1))
        ring = ctx.enter_context(tc.tile_pool(name="ring", bufs=4))
        psum_h = ctx.enter_context(tc.psum_pool(name="psum_h", bufs=5))
        psum_y = ctx.enter_context(tc.psum_pool(name="psum_y", bufs=1))

        offsets = keep.tile([P, S // LIST_ROWS], U16, name="offsets")
        nc.sync.dma_start(offsets[:], offs)

        all_scales = keep.tile([P, T], U8, name="all_scales", align_bytes=64)
        nc.gpsimd.memset(all_scales[:, 0 : T // 2].bitcast(I32), 0)
        nc.vector.memset(all_scales[:, T // 2 : T].bitcast(I32), 0)


        w1_rows = w1.rearrange("(p j) c -> p j c", j=PACK)
        half = PASS // 2
        w1_first = []
        for u in range(2):
            raw = keep.tile([P, PACK, half], F32, name=f"w1_first{u}")
            nc.sync.dma_start(raw[:], w1_rows[:, :, u * half : (u + 1) * half])
            w1_first.append(raw)
            if u == 0:
                for q in range(4):
                    nc.sync.dma_start(all_scales[32 * q : 32 * q + 4, :].bitcast(I32), x_scales[0, 4 * q : 4 * q + 4, :].bitcast(I32))
        all_words = keep.tile([P, T], I32, name="all_words", align_bytes=64)
        nc.sync.dma_start(all_words[:], x_words[0].rearrange("p c r -> p (c r)").bitcast(I32))
        w1_second = []
        for u in range(2):
            raw = keep.tile([P, PACK, half], F32, name=f"w1_second{u}", tag=f"w1_second{u}", align_bytes=64)
            nc.sync.dma_start(raw[:], w1_rows[:, :, PASS + u * half : PASS + (u + 1) * half])
            w1_second.append(raw)
        w2_raw = []
        for g in range(PASSES):
            raw = keep.tile([P, PACK, N], F32, name=f"w2_raw{g}", tag=f"w2_raw{g}", align_bytes=64)
            nc.sync.dma_start(raw[:], w2[g * PASS : (g + 1) * PASS, :].rearrange("(p j) n -> p j n", j=PACK))
            w2_raw.append(raw)
        gates = keep.tile([P, S], F32, name="gates")
        nc.sync.dma_start(gates[:], gate[0:P, :])

        windows = []
        for m in range(ROW_TILES):
            window = keep.tile([P, T], F32, name=f"window{m}")
            nc.vector.memset(window[:], 0.0)
            windows.append(window)

        picked_scales = keep.tile([P, S], U8, name="picked_scales", align_bytes=64)
        nc.vector.tensor_copy(picked_scales[:], all_scales[:].indirect(offsets[:]))

        w1_grouped = [keep.tile([P, PACK, P, PACK], BF16, name=f"w1_grouped{g}", align_bytes=64) for g in range(PASSES)]
        w1_codes = [keep.tile([P, PASS], U32, name=f"w1_codes{g}", align_bytes=64) for g in range(PASSES)]
        w1_planes = [keep.tile([P, PASS], U8, name=f"w1_planes{g}", align_bytes=64) for g in range(PASSES)]

        def quantize_w1(g):
            nc.vector.quantize_mx(
                out=w1_codes[g][:].bitcast(FP8X4),
                scales=w1_planes[g][:],
                in_=w1_grouped[g][:].rearrange("p t m j -> p (t m j)"),
            )

        for u in range(2):
            nc.scalar.copy(
                w1_grouped[0][:, :, u * (P // 2) : (u + 1) * (P // 2), :].rearrange("p t m j -> p m j t"),
                w1_first[u][:].rearrange("p j (m t) -> p m j t", t=PACK),
            )
        quantize_w1(0)

        def chunk_offsets(c):
            return offsets[:, c * (CHUNK // LIST_ROWS) : (c + 1) * (CHUNK // LIST_ROWS)]

        picked_words = {}

        def pick_words(c, tag):
            words = keep.tile([P, CHUNK], U32, name=f"picked_words{c}", tag=tag, align_bytes=64)
            nc.vector.tensor_copy(words[:], all_words[:].bitcast(U32).indirect(chunk_offsets(c)))
            picked_words[c] = words

        pick_words(0, "picked_words0")
        pick_words(1, "picked_words1")
        for u in range(2):
            nc.vector.tensor_copy(
                w1_grouped[1][:, :, u * (P // 2) : (u + 1) * (P // 2), :].rearrange("p t m j -> p m j t"),
                w1_second[u][:].rearrange("p j (m t) -> p m j t", t=PACK),
            )
        quantize_w1(1)
        pick_words(2, "picked_words2")

        w2_codes, w2_planes = [], []
        for g in range(PASSES):
            grouped = keep.tile([P, N, PACK], BF16, name=f"w2_grouped{g}", align_bytes=64)
            nc.vector.tensor_copy(
                grouped[:].rearrange("p (n i) j -> p n j i", i=4),
                w2_raw[g][:].rearrange("p j (n i) -> p n j i", i=4),
            )
            codes = keep.tile([P, N], U32, name=f"w2_codes{g}", align_bytes=64)
            plane = keep.tile([P, N], U8, name=f"w2_plane{g}", align_bytes=64)
            nc.vector.quantize_mx(out=codes[:].bitcast(FP8X4), scales=plane[:], in_=grouped[:].rearrange("p n j -> p (n j)"))
            w2_codes.append(codes)
            w2_planes.append(plane)
        pick_words(3, "w2_raw1")

        def put_back(c, m, y, staged):
            nc.scalar.copy(staged[:], y[:])
            nc.vector.tensor_tensor(windows[m][:].indirect(chunk_offsets(c)), staged[:], gates[:, c * CHUNK : (c + 1) * CHUNK], ALU.mult)

        on_vector = [[0, 512], [512, 0], [512, 0], [512, 0]]
        width = CHUNK * PACK
        held = None
        for c in range(CHUNKS):
            ys = [psum_y.tile([P, CHUNK], F32, name="y0", bufs=1), psum_y.tile([P, CHUNK], F32, name="y1", bufs=2)]
            for g in range(PASSES):
                if g == PASSES - 1:
                    positive = keep.tile([P, CHUNK, PACK], F32, name="positive_last", tag=f"shared{c % 2}")
                else:
                    positive = ring.tile([P, CHUNK, PACK], F32, name="positive")
                for a in range(CHUNK // UNIT):
                    cols = slice(a * UNIT, (a + 1) * UNIT)
                    entries = slice(c * CHUNK + a * UNIT, c * CHUNK + (a + 1) * UNIT)
                    pre = psum_h.tile([P, PACK, UNIT], F32, name="pre")
                    for t in range(PACK):
                        nc.tensor.matmul_mx(
                            out=pre[:, t, :],
                            lhsT=w1_codes[g][:, t * P : (t + 1) * P].bitcast(FP8X4),
                            lhsT_scale=w1_planes[g][:, t * P : (t + 1) * P],
                            rhs=picked_words[c][:, cols].bitcast(FP8X4),
                            rhs_scale=picked_scales[:, entries],
                            start=True,
                            stop=True,
                        )
                    nc.scalar.activation(positive[:, cols, :], pre[:].rearrange("p t n -> p n t"), ACT.Relu)
                flat = positive[:].rearrange("p n t -> p (n t)")
                hidden = keep.tile([P, width], BF16, name=f"hidden{c}_{g}", align_bytes=64)
                share = on_vector[c][g]
                if share > 0:
                    nc.vector.tensor_tensor(hidden[:, 0:share], flat[:, 0:share], flat[:, 0:share], ALU.mult)
                if share < width:
                    nc.scalar.activation(hidden[:, share:width], flat[:, share:width], ACT.Square)
                codes = keep.tile([P, CHUNK], U32, name=f"h_codes{c}_{g}", align_bytes=64)
                plane = keep.tile([P, CHUNK], U8, name=f"h_plane{c}_{g}", align_bytes=64)
                nc.vector.quantize_mx(out=codes[:].bitcast(FP8X4), scales=plane[:], in_=hidden[:])
                for m in range(ROW_TILES):
                    nc.tensor.matmul_mx(
                        out=ys[m][:],
                        lhsT=w2_codes[g][:, m * P : (m + 1) * P].bitcast(FP8X4),
                        lhsT_scale=w2_planes[g][:, m * P : (m + 1) * P],
                        rhs=codes[:].bitcast(FP8X4),
                        rhs_scale=plane[:],
                        start=(g == 0),
                        stop=(g == PASSES - 1),
                    )
            if held is not None:
                put_back(c - 1, 1, held, keep.tile([P, CHUNK], F32, name="staged_held", tag=f"shared{c % 2}"))
            put_back(c, 0, ys[0], ring.tile([P, CHUNK], F32, name="staged"))
            held = ys[1]
        put_back(CHUNKS - 1, 1, held, ring.tile([P, CHUNK], F32, name="staged"))

        for m in range(ROW_TILES):
            nc.sync.dma_start(out[m * P : (m + 1) * P, :], windows[m][:])
